import numpy as np
CORES = [32,33,34,35,40,41,42,43]
N = 8
def setup_inputs(rng):
    return {"x": rng.standard_normal((N, 128, 256), dtype=np.float32)}
def reference(x):
    g = np.concatenate(list(x), axis=1)
    return {"y": np.broadcast_to(g, (N,) + g.shape)}

@@ -1,0 +1,144 @@
+from concourse.bass import DstId, RemoteDMATransfer
+
+N = 8
+W = 256
+P = 2
+OWN = "first"
+LATE = "pipe"
+EARLY_PIECES = True
+LATE_STORE = "piece"
+ROTATE = True
+
+SCRATCH = {
+    "d": ("dram", [N * P, 128, W // P], "float32"),
+}
+SEMAPHORES = (["sent", "stored"] + ["ld%d" % c for c in range(P)] + ["a%d" % s for s in range(N * P)])
+
+
+def rot(lst, n):
+    if not ROTATE:
+        return list(lst)
+    n = n % len(lst)
+    return list(lst[n:]) + list(lst[:n])
+
+
+def route(cores, j):
+    s = cores[j]
+    k = s % 8
+    b = s - k
+    o = 8 * ((s // 8) ^ 1)
+    mine = [c for c in cores if c // 8 == s // 8]
+    peers = rot(mine, k + 1)[:len(mine) - 1] if ROTATE else [c for c in mine if c != s]
+    far = [c for c in cores if c // 8 != s // 8]
+    hops = []
+    local = [(c, peers) for c in range(P)]
+    if k < 2:
+        gw = b + 6 + k
+        fan = [o + (6 if c % 2 == 0 else 4) + k for c in range(P)]
+        if LATE == "two":
+            via = b + 2 + k
+            hops += [(0.0, s, [(0, [gw])]), (0.01, s, [(1, [via])]),
+                     (1.0, gw, [(0, [fan[0]])]), (1.01, via, [(1, [fan[1]])])]
+            local = [(0, peers), (1, [p for p in peers if p != via])]
+        elif LATE == "pipe":
+            for c in range(P):
+                hops += [(0.0 + c / 100, s, [(c, [gw])]), (1.0 + c / 100, gw, [(c, [fan[c]])])]
+        else:
+            hops += [(0.0, s, [(c, [gw]) for c in range(P)]), (1.0, gw, [(c, [fan[c]]) for c in range(P)])]
+        for c in range(P):
+            hops.append((2.0 + c / 100, fan[c], [(c, rot(far, 2 * c + k))]))
+    else:
+        fan = o + 2 + k
+        if EARLY_PIECES:
+            for c in range(P):
+                hops += [(0.0 + c / 100, s, [(c, [fan])]), (1.0 + c / 100, fan, [(c, rot(far, 2 * k))])]
+        else:
+            hops += [(0.0, s, [(c, [fan]) for c in range(P)]), (1.0, fan, [(c, rot(far, 2 * k)) for c in range(P)])]
+    hops.append((0.5, s, local))
+    return hops
+
+
+def rank_program(g, core, T, topo):
+    cores = list(T.cores)
+    rank = T.rank_of(core)
+    hops = [(h, j) for j in range(N) for h in route(cores, j)]
+    pieces_load = LATE != "par" or EARLY_PIECES
+
+    def engines(h):
+        total = 16 if h[2][0][1][0] // 8 == h[1] // 8 else 8
+        return total // len(h[2])
+
+    count = {}
+    groups = {}
+    for h, j in hops:
+        got = [c for c, dsts in h[2] if core in dsts]
+        if not got:
+            continue
+        for c in got:
+            count[j * P + c] = engines(h)
+        pos = [dsts.index(core) for c, dsts in h[2] if core in dsts][0]
+        lev, key = int(h[0]), h[0] + pos / 10
+        name = (j, got[0]) if (lev > 0 and LATE_STORE == "piece") else j
+        if name in groups:
+            groups[name] = [lev, max(groups[name][1], key), j, sorted(groups[name][3] + got)]
+        else:
+            groups[name] = [lev, key, j, got]
+    sends = sorted([(h[0], j, h) for h, j in hops if h[1] == core])
+    if not sends and not groups:
+        return
+
+    rows = 128 // P
+    nstores = 0
+
+    if rank is not None:
+        if pieces_load:
+            for c in range(P):
+                q = [g.sync, g.scalar][c % 2]
+                q.dma_start(T.d[rank * P + c], T.x[c * rows:(c + 1) * rows, :]).then_inc(T.sem["ld%d" % c], 16)
+        else:
+            g.sync.dma_start(T.d[rank * P:(rank + 1) * P], T.x[:, :]).then_inc(T.sem.ld0, 16)
+        if OWN == "first":
+            g.scalar.dma_start(T.y[:, rank * W:(rank + 1) * W], T.x[:, :]).then_inc(T.sem.stored, 16)
+            nstores += 1
+
+    sent = 0
+    for key, j, h in sends:
+        eng = engines(h)
+        trs = []
+        for n, (c, dsts) in enumerate(h[2]):
+            slot = j * P + c
+            if j == rank:
+                g.wait_ge(T.sem["ld%d" % (c if pieces_load else 0)], 16)
+            else:
+                g.wait_ge(T.sem["a%d" % slot], count[slot])
+            ids = []
+            for dcore in dsts:
+                rid, pid, se = topo.addr(dcore)
+                ids.append(DstId(rid=rid, pnc=pid))
+            mask = ((1 << eng) - 1) << (n * eng)
+            trs.append(RemoteDMATransfer(dst_ids=ids, dma_engine_mask=mask, remote_sem=T.sem["a%d" % slot],
+                                         srcs=[T.d[slot]], dsts=[T.d[slot] for dcore in dsts]))
+            sent += eng
+        g.remote_dma_fused(trs, local_sem=T.sem.sent)
+
+    if rank is not None:
+        queues = [g.sync, g.scalar]
+        turn = 0
+        if OWN == "sent":
+            g.scalar.wait_ge(T.sem.sent, sent)
+            g.scalar.dma_start(T.y[:, rank * W:(rank + 1) * W], T.x[:, :]).then_inc(T.sem.stored, 16)
+            nstores += 1
+        for lev, key, j, pieces in sorted(groups.values()):
+            q = queues[turn % 2]
+            turn += 1
+            for c in pieces:
+                q.wait_ge(T.sem["a%d" % (j * P + c)], count[j * P + c])
+            lo, hi = pieces[0], pieces[-1] + 1
+            q.dma_start(T.y[lo * rows:hi * rows, j * W:(j + 1) * W],
+                        T.d[j * P + lo:j * P + hi]).then_inc(T.sem.stored, 16)
+            nstores += 1
+
+    if sent:
+        g.wait_ge(T.sem.sent, sent)
+    if nstores:
+        g.wait_ge(T.sem.stored, 16 * nstores)

@@ -3,11 +3,8 @@ from concourse.bass import DstId, RemoteDMATransfer
 N = 8
 W = 256
 P = 2
-OWN = "first"
-LATE = "pipe"
-EARLY_PIECES = True
-LATE_STORE = "piece"
-ROTATE = True
+LATE_CALLS = [[0], [1]]
+EARLY_CALLS = [[0], [1]]
 
 SCRATCH = {
     "d": ("dram", [N * P, 128, W // P], "float32"),
@@ -16,8 +13,6 @@ SEMAPHORES = (["sent", "stored"] + ["ld%d" % c for c in range(P)] + ["a%d" % s f
 
 
 def rot(lst, n):
-    if not ROTATE:
-        return list(lst)
     n = n % len(lst)
     return list(lst[n:]) + list(lst[:n])
 
@@ -28,33 +23,21 @@ def route(cores, j):
     b = s - k
     o = 8 * ((s // 8) ^ 1)
     mine = [c for c in cores if c // 8 == s // 8]
-    peers = rot(mine, k + 1)[:len(mine) - 1] if ROTATE else [c for c in mine if c != s]
+    peers = rot(mine, k + 1)[:len(mine) - 1]
     far = [c for c in cores if c // 8 != s // 8]
     hops = []
-    local = [(c, peers) for c in range(P)]
     if k < 2:
         gw = b + 6 + k
-        fan = [o + (6 if c % 2 == 0 else 4) + k for c in range(P)]
-        if LATE == "two":
-            via = b + 2 + k
-            hops += [(0.0, s, [(0, [gw])]), (0.01, s, [(1, [via])]),
-                     (1.0, gw, [(0, [fan[0]])]), (1.01, via, [(1, [fan[1]])])]
-            local = [(0, peers), (1, [p for p in peers if p != via])]
-        elif LATE == "pipe":
-            for c in range(P):
-                hops += [(0.0 + c / 100, s, [(c, [gw])]), (1.0 + c / 100, gw, [(c, [fan[c]])])]
-        else:
-            hops += [(0.0, s, [(c, [gw]) for c in range(P)]), (1.0, gw, [(c, [fan[c]]) for c in range(P)])]
-        for c in range(P):
-            hops.append((2.0 + c / 100, fan[c], [(c, rot(far, 2 * c + k))]))
+        for n, grp in enumerate(LATE_CALLS):
+            fan = o + (6 if n % 2 == 0 else 4) + k
+            hops += [(0.0 + n / 100, s, [(c, [gw]) for c in grp]), (1.0 + n / 100, gw, [(c, [fan]) for c in grp]),
+                     (2.0 + n / 100, fan, [(c, rot(far, 2 * n + k)) for c in grp])]
+        hops.append((0.5, s, [(c, peers) for c in range(P)]))
     else:
         fan = o + 2 + k
-        if EARLY_PIECES:
-            for c in range(P):
-                hops += [(0.0 + c / 100, s, [(c, [fan])]), (1.0 + c / 100, fan, [(c, rot(far, 2 * k))])]
-        else:
-            hops += [(0.0, s, [(c, [fan]) for c in range(P)]), (1.0, fan, [(c, rot(far, 2 * k)) for c in range(P)])]
-    hops.append((0.5, s, local))
+        for n, grp in enumerate(EARLY_CALLS):
+            hops += [(0.0 + n / 100, s, [(c, [fan]) for c in grp] + [(c, peers) for c in grp]),
+                     (1.0 + n / 100, fan, [(c, rot(far, 2 * k)) for c in grp])]
     return hops
 
 
@@ -62,11 +45,10 @@ def rank_program(g, core, T, topo):
     cores = list(T.cores)
     rank = T.rank_of(core)
     hops = [(h, j) for j in range(N) for h in route(cores, j)]
-    pieces_load = LATE != "par" or EARLY_PIECES
 
     def engines(h):
-        total = 16 if h[2][0][1][0] // 8 == h[1] // 8 else 8
-        return total // len(h[2])
+        away = [dsts[0] // 8 != h[1] // 8 for c, dsts in h[2]]
+        return (8 if all(away) else 16) // len(h[2])
 
     count = {}
     groups = {}
@@ -77,12 +59,7 @@ def rank_program(g, core, T, topo):
         for c in got:
             count[j * P + c] = engines(h)
         pos = [dsts.index(core) for c, dsts in h[2] if core in dsts][0]
-        lev, key = int(h[0]), h[0] + pos / 10
-        name = (j, got[0]) if (lev > 0 and LATE_STORE == "piece") else j
-        if name in groups:
-            groups[name] = [lev, max(groups[name][1], key), j, sorted(groups[name][3] + got)]
-        else:
-            groups[name] = [lev, key, j, got]
+        groups[(j, got[0])] = [int(h[0]), h[0] + pos / 10, j, got]
     sends = sorted([(h[0], j, h) for h, j in hops if h[1] == core])
     if not sends and not groups:
         return
@@ -90,16 +67,16 @@ def rank_program(g, core, T, topo):
     rows = 128 // P
     nstores = 0
 
+    ldsem = {}
     if rank is not None:
-        if pieces_load:
-            for c in range(P):
-                q = [g.sync, g.scalar][c % 2]
-                q.dma_start(T.d[rank * P + c], T.x[c * rows:(c + 1) * rows, :]).then_inc(T.sem["ld%d" % c], 16)
-        else:
-            g.sync.dma_start(T.d[rank * P:(rank + 1) * P], T.x[:, :]).then_inc(T.sem.ld0, 16)
-        if OWN == "first":
-            g.scalar.dma_start(T.y[:, rank * W:(rank + 1) * W], T.x[:, :]).then_inc(T.sem.stored, 16)
-            nstores += 1
+        for n, grp in enumerate(LATE_CALLS if core % 8 < 2 else EARLY_CALLS):
+            q = [g.sync, g.scalar][n % 2]
+            lo, hi = grp[0], grp[-1] + 1
+            q.dma_start(T.d[rank * P + lo:rank * P + hi], T.x[lo * rows:hi * rows, :]).then_inc(T.sem["ld%d" % n], 16)
+            for c in grp:
+                ldsem[c] = T.sem["ld%d" % n]
+        g.scalar.dma_start(T.y[:, rank * W:(rank + 1) * W], T.x[:, :]).then_inc(T.sem.stored, 16)
+        nstores += 1
 
     sent = 0
     for key, j, h in sends:
@@ -108,7 +85,7 @@ def rank_program(g, core, T, topo):
         for n, (c, dsts) in enumerate(h[2]):
             slot = j * P + c
             if j == rank:
-                g.wait_ge(T.sem["ld%d" % (c if pieces_load else 0)], 16)
+                g.wait_ge(ldsem[c], 16)
             else:
                 g.wait_ge(T.sem["a%d" % slot], count[slot])
             ids = []
@@ -124,10 +101,6 @@ def rank_program(g, core, T, topo):
     if rank is not None:
         queues = [g.sync, g.scalar]
         turn = 0
-        if OWN == "sent":
-            g.scalar.wait_ge(T.sem.sent, sent)
-            g.scalar.dma_start(T.y[:, rank * W:(rank + 1) * W], T.x[:, :]).then_inc(T.sem.stored, 16)
-            nstores += 1
         for lev, key, j, pieces in sorted(groups.values()):
             q = queues[turn % 2]
             turn += 1

from concourse.bass import DstId, RemoteDMATransfer

N = 8
W = 256
P = 2
LATE_CALLS = [[0], [1]]
EARLY_CALLS = [[0], [1]]

SCRATCH = {
    "d": ("dram", [N * P, 128, W // P], "float32"),
}
SEMAPHORES = (["sent", "stored"] + ["ld%d" % c for c in range(P)] + ["a%d" % s for s in range(N * P)])


def rot(lst, n):
    n = n % len(lst)
    return list(lst[n:]) + list(lst[:n])


def route(cores, j):
    s = cores[j]
    k = s % 8
    b = s - k
    o = 8 * ((s // 8) ^ 1)
    mine = [c for c in cores if c // 8 == s // 8]
    peers = rot(mine, k + 1)[:len(mine) - 1]
    far = [c for c in cores if c // 8 != s // 8]
    hops = []
    if k < 2:
        gw = b + 6 + k
        for n, grp in enumerate(LATE_CALLS):
            fan = o + (6 if n % 2 == 0 else 4) + k
            hops += [(0.0 + n / 100, s, [(c, [gw]) for c in grp]), (1.0 + n / 100, gw, [(c, [fan]) for c in grp]),
                     (2.0 + n / 100, fan, [(c, rot(far, 2 * n + k)) for c in grp])]
        hops.append((0.5, s, [(c, peers) for c in range(P)]))
    else:
        fan = o + 2 + k
        for n, grp in enumerate(EARLY_CALLS):
            hops += [(0.0 + n / 100, s, [(c, [fan]) for c in grp] + [(c, peers) for c in grp]),
                     (1.0 + n / 100, fan, [(c, rot(far, 2 * k)) for c in grp])]
    return hops


def rank_program(g, core, T, topo):
    cores = list(T.cores)
    rank = T.rank_of(core)
    hops = [(h, j) for j in range(N) for h in route(cores, j)]

    def engines(h):
        away = [dsts[0] // 8 != h[1] // 8 for c, dsts in h[2]]
        return (8 if all(away) else 16) // len(h[2])

    count = {}
    groups = {}
    for h, j in hops:
        got = [c for c, dsts in h[2] if core in dsts]
        if not got:
            continue
        for c in got:
            count[j * P + c] = engines(h)
        pos = [dsts.index(core) for c, dsts in h[2] if core in dsts][0]
        groups[(j, got[0])] = [int(h[0]), h[0] + pos / 10, j, got]
    sends = sorted([(h[0], j, h) for h, j in hops if h[1] == core])
    if not sends and not groups:
        return

    rows = 128 // P
    nstores = 0

    ldsem = {}
    if rank is not None:
        for n, grp in enumerate(LATE_CALLS if core % 8 < 2 else EARLY_CALLS):
            q = [g.sync, g.scalar][n % 2]
            lo, hi = grp[0], grp[-1] + 1
            q.dma_start(T.d[rank * P + lo:rank * P + hi], T.x[lo * rows:hi * rows, :]).then_inc(T.sem["ld%d" % n], 16)
            for c in grp:
                ldsem[c] = T.sem["ld%d" % n]
        g.scalar.dma_start(T.y[:, rank * W:(rank + 1) * W], T.x[:, :]).then_inc(T.sem.stored, 16)
        nstores += 1

    sent = 0
    for key, j, h in sends:
        eng = engines(h)
        trs = []
        for n, (c, dsts) in enumerate(h[2]):
            slot = j * P + c
            if j == rank:
                g.wait_ge(ldsem[c], 16)
            else:
                g.wait_ge(T.sem["a%d" % slot], count[slot])
            ids = []
            for dcore in dsts:
                rid, pid, se = topo.addr(dcore)
                ids.append(DstId(rid=rid, pnc=pid))
            mask = ((1 << eng) - 1) << (n * eng)
            trs.append(RemoteDMATransfer(dst_ids=ids, dma_engine_mask=mask, remote_sem=T.sem["a%d" % slot],
                                         srcs=[T.d[slot]], dsts=[T.d[slot] for dcore in dsts]))
            sent += eng
        g.remote_dma_fused(trs, local_sem=T.sem.sent)

    if rank is not None:
        queues = [g.sync, g.scalar]
        turn = 0
        for lev, key, j, pieces in sorted(groups.values()):
            q = queues[turn % 2]
            turn += 1
            for c in pieces:
                q.wait_ge(T.sem["a%d" % (j * P + c)], count[j * P + c])
            lo, hi = pieces[0], pieces[-1] + 1
            q.dma_start(T.y[lo * rows:hi * rows, j * W:(j + 1) * W],
                        T.d[j * P + lo:j * P + hi]).then_inc(T.sem.stored, 16)
            nstores += 1

    if sent:
        g.wait_ge(T.sem.sent, sent)
    if nstores:
        g.wait_ge(T.sem.stored, 16 * nstores)
